import numpy as np
import ml_dtypes


def mxq(x, axis, fmt="e4m3"):
    dtype, down = {"e4m3": (ml_dtypes.float8_e4m3fn, 7), "e5m2": (ml_dtypes.float8_e5m2, 14)}[fmt]
    v = np.moveaxis(np.asarray(x, np.float32).astype(ml_dtypes.bfloat16).astype(np.float64), axis, -1)
    blocks = v.reshape(v.shape[:-1] + (-1, 32))
    amax = np.abs(blocks).max(-1, keepdims=True)
    byte = np.maximum(np.where(amax > 0, np.frexp(amax)[1] - 1 + 127, 0) - down, 1)
    scale = np.exp2(byte - 127.0)
    codes = (blocks / scale).astype(np.float32).astype(dtype).astype(np.float64)
    return np.moveaxis((codes * scale).reshape(v.shape), -1, axis)


WIDE = False


def mx_kscale(k):
    if not WIDE:
        return np.ones(k)
    levels = np.array([10, -10, 5, -5, 0])
    if k % 512:
        return np.exp2(np.random.permutation(np.resize(levels, k // 32))).repeat(32)
    a = np.empty((k // 512, 16))
    for p in range(k // 512):
        a[p, :8] = np.random.permutation(np.resize(levels, 8))
        for g in range(8):
            far = levels[np.abs(levels - a[p, g]) >= 10]
            a[p, g + 8] = far[np.random.randint(len(far))]
    return np.exp2(a.ravel()).repeat(32)


def f64(x):
    return np.asarray(x).astype(np.float64)


def striped(idx):
    return np.tile(idx.reshape(-1, 16).T, (8, 1)).astype(np.uint16)


def unstriped(offs):
    return offs[:16].T.reshape(-1).astype(np.int64)


E2M1 = np.array([0.0, 0.5, 1.0, 1.5, 2.0, 3.0, 4.0, 6.0, -0.0, -0.5, -1.0, -1.5, -2.0, -3.0, -4.0, -6.0])


def pack_weight(w, fmt):
    k, n = w.shape
    w = f64(np.asarray(w, np.float32).astype(ml_dtypes.bfloat16)).reshape(k // 32, 32, n)
    amax = np.abs(w).max(1)
    if fmt == "e4m3":
        byte = np.frexp(amax)[1] - 1 + 127 - 7
    else:
        mant, ex = np.frexp(amax / 6.0)
        byte = np.where(mant > 0.5, ex, ex - 1) + 127
    byte = np.clip(np.where(amax > 0, byte, 1), 1, 254)
    scaled = (w * np.exp2(127.0 - byte)[:, None, :]).reshape(k, n).astype(np.float32)
    by_word = np.ascontiguousarray(scaled.reshape(k // 512, 128, 4, n).transpose(0, 1, 3, 2))
    if fmt == "e4m3":
        words = by_word.astype(ml_dtypes.float8_e4m3fn).view(np.uint8)
    else:
        c = by_word.astype(ml_dtypes.float4_e2m1fn).view(np.uint8) & 0xF
        words = (c[..., 0::2] | (c[..., 1::2] << 4)).reshape(k // 512, 128, 2 * n)
    return np.ascontiguousarray(words), np.ascontiguousarray(byte.astype(np.uint8).reshape(k // 512, 16, n))


def unpack_weight(words, scales, fmt):
    g, _, n = scales.shape
    words = np.ascontiguousarray(words).reshape(g, 128, n, -1)
    if fmt == "e4m3":
        vals = words.view(ml_dtypes.float8_e4m3fn).astype(np.float64)
    else:
        nib = np.empty((g, 128, n, 4), np.uint8)
        nib[..., 0::2] = words & 0xF
        nib[..., 1::2] = words >> 4
        vals = E2M1[nib]
    vals = vals * np.repeat(np.exp2(scales.astype(np.float64) - 127.0), 8, axis=1)[..., None]
    return vals.transpose(0, 1, 3, 2).reshape(g * 512, n)


def gelu(v):
    return 0.5 * v * (1.0 + np.tanh(np.sqrt(2.0 / np.pi) * (v + 0.044715 * v**3)))


def bf(x):
    return np.asarray(x, np.float32).astype(ml_dtypes.bfloat16)


def planes(Y):
    n, m = Y.shape
    b = f64(bf(Y)).reshape(n // 32, 32, m)
    amax = np.abs(b).max(1)
    byte = np.clip(np.where(amax > 0, np.frexp(amax)[1] - 1 + 127 - 7, 1), 1, 254)
    codes = (b * np.exp2(127.0 - byte)[:, None, :]).reshape(n, m).astype(np.float32).astype(ml_dtypes.float8_e4m3fn).view(np.uint8)
    words = codes.reshape(n // 512, 128, 4, m).transpose(0, 1, 3, 2)
    return np.ascontiguousarray(words), np.ascontiguousarray(byte.astype(np.uint8).reshape(n // 512, 16, m))


K, K2, H, N, T, S = 1024, 512, 1024, 512, 4096, 1024


def setup_inputs():
    n = np.random.standard_normal
    s = mx_kscale(K)[:, None]
    s2 = mx_kscale(K2)[:, None]
    u = mx_kscale(H)[:, None]
    d = {}
    d["tab_words"], d["tab_scales"] = pack_weight(n((K, T)) * s, "e4m3")
    d["offs"] = striped(np.random.permutation(T)[:S])
    d["xs_words"], d["xs_scales"] = pack_weight(n((K2, S)) * s2, "e4m3")
    d["w1"] = (1.3 * n((K, H)) / K ** 0.5 / s * u.T).astype(np.float32)
    d["w2_words"], d["w2_scales"] = pack_weight(0.8 * n((K2, H)) / K2 ** 0.5 / s2 * u.T, "e2m1")
    d["lo"] = (-(0.2 + 0.9 * np.random.uniform(0.0, 1.0, H)) * u[:, 0]).astype(np.float32)
    d["hi"] = ((0.3 + 1.0 * np.random.uniform(0.0, 1.0, H)) * u[:, 0]).astype(np.float32)
    d["w3"] = (n((H, N)) / H ** 0.5 / u * np.exp(0.8 * n(N))).astype(np.float32)
    return d


def reference(tab_words, tab_scales, offs, xs_words, xs_scales, w1, w2_words, w2_scales, lo, hi, w3):
    v = unpack_weight(tab_words, tab_scales, "e4m3")[:, unstriped(offs)]
    xs = unpack_weight(xs_words, xs_scales, "e4m3")
    w2 = unpack_weight(w2_words, w2_scales, "e2m1")
    water = mxq(f64(w1), 0, "e4m3").T @ v
    raised = np.maximum(water, f64(lo)[:, None])
    held = np.minimum(raised, f64(hi)[:, None])
    lamp = w2.T @ xs
    h = held - lamp
    y = mxq(f64(w3), 0, "e4m3").T @ mxq(h, 0, "e4m3")
    words, scales = planes(y)
    return y, words, scales

@@ -1,0 +1,211 @@
+from contextlib import ExitStack
+
+import concourse.mybir as mybir
+
+K, K2, H, N, T, S = 1024, 512, 1024, 512, 4096, 1024
+FLOPS = 2 * S * (K * H + K2 * H + H * N)
+
+F32 = mybir.dt.float32
+BF16 = mybir.dt.bfloat16
+I32 = mybir.dt.int32
+U32 = mybir.dt.uint32
+U16 = mybir.dt.uint16
+U8 = mybir.dt.uint8
+FP8X4 = mybir.dt.float8_e4m3fn_x4
+FP4X4 = mybir.dt.float4_e2m1fn_x4
+ALU = mybir.AluOpType
+
+P = 128
+PASS = 512
+HALF = 512
+VIA_SCALAR = {(0, 0, 3), (0, 1, 2), (0, 1, 3), (1, 0, 2), (1, 0, 3), (1, 1, 1), (1, 1, 2), (1, 1, 3)}
+Y_CHUNKS = ((0, 256), (256, 256), (512, 256), (768, 128), (896, 128))
+Y_CAST_ON_SCALAR = (0, 256)
+
+
+def tile_list_ballast_kill_encoder_kernel(
+    tc, tab_words, tab_scales, offs, xs_words, xs_scales, w1, w2_words, w2_scales, lo, hi, w3, out_0, out_1, out_2
+):
+    nc = tc.nc
+    with ExitStack() as ctx:
+        keep = ctx.enter_context(tc.tile_pool(name="keep", bufs=1))
+        ring = ctx.enter_context(tc.tile_pool(name="ring", bufs=2))
+        psum = ctx.enter_context(tc.psum_pool(name="psum", bufs=1))
+
+        def kept(shape, dtype, name):
+            return keep.tile(shape, dtype, name=name, align_bytes=64)
+
+        offsets = kept([P, S // 16], U16, "offsets")
+        tab_w = [kept([P, T], U32, "tab_w%d" % a) for a in range(2)]
+        tab_s = kept([P, T], U8, "tab_s")
+        xs_w = kept([P, S], U32, "xs_w")
+        xs_s = kept([P, S], U8, "xs_s")
+        w2_raw = kept([P, 2 * H], U8, "w2_raw")
+        w2_s_raw = kept([P, H], U8, "w2_s_raw")
+        lo_sb = kept([P, 2, 4], F32, "lo_sb")
+        hi_sb = kept([P, 2, 4], F32, "hi_sb")
+        w1_raw = [[kept([P, 4, PASS], F32, "w1_raw%d%d" % (b, a)) for a in range(2)] for b in range(2)]
+        w3_raw = [kept([P, 4, N], F32, "w3_raw%d" % b) for b in range(2)]
+
+        for plane in (tab_s, w2_s_raw, xs_s):
+            nc.vector.memset(plane[:].bitcast(I32), 0)
+
+        def load_w1(b, a):
+            rows = w1[PASS * a : PASS * (a + 1), PASS * b : PASS * (b + 1)]
+            nc.sync.dma_start(w1_raw[b][a][:], rows.rearrange("(p j) c -> p j c", j=4))
+
+        def load_words(tile, words):
+            nc.sync.dma_start(tile[:].bitcast(I32), words.rearrange("p c i -> p (c i)").bitcast(I32))
+
+        load_words(tab_w[0], tab_words[0])
+        nc.sync.dma_start(offsets[:], offs)
+        for q in range(4):
+            nc.sync.dma_start(tab_s[32 * q : 32 * q + 8, :].bitcast(I32), tab_scales[:, 4 * q : 4 * q + 4, :].bitcast(I32))
+        nc.scalar.dma_start(w2_raw[:].bitcast(I32), w2_words[0].bitcast(I32))
+        load_words(tab_w[1], tab_words[1])
+        load_w1(0, 0)
+        load_w1(0, 1)
+        load_words(xs_w, xs_words[0])
+        load_w1(1, 0)
+        load_w1(1, 1)
+        for b in range(2):
+            nc.sync.dma_start(w3_raw[b][:], w3[PASS * b : PASS * (b + 1), :].rearrange("(p j) n -> p j n", j=4))
+
+        for q in range(4):
+            nc.gpsimd.dma_start(w2_s_raw[32 * q : 32 * q + 4, :].bitcast(I32), w2_scales[0, 4 * q : 4 * q + 4, :].bitcast(I32))
+        nc.gpsimd.dma_start(lo_sb[:], lo.rearrange("(b p t) -> p b t", b=2, t=4))
+        nc.gpsimd.dma_start(hi_sb[:], hi.rearrange("(b p t) -> p b t", b=2, t=4))
+        for q in range(4):
+            nc.gpsimd.dma_start(xs_s[32 * q : 32 * q + 4, :].bitcast(I32), xs_scales[0, 4 * q : 4 * q + 4, :].bitcast(I32))
+
+        w2_w = kept([P, 2 * H], U8, "w2_w")
+        w2_s = kept([P, H], U8, "w2_s")
+        nc.vector.tensor_copy(
+            w2_w[:].rearrange("p (b t m e) -> p b t m e", b=2, t=4, e=2),
+            w2_raw[:].rearrange("p (b m t e) -> p b t m e", b=2, t=4, e=2),
+        )
+
+        v_w = [kept([P, S], U32, "v_w%d" % a) for a in range(2)]
+        v_s = kept([P, S], U8, "v_s")
+        nc.vector.tensor_copy(v_w[0][:], tab_w[0][:].indirect(offsets[:]))
+        nc.vector.tensor_copy(v_s[:], tab_s[:].indirect(offsets[:]))
+        nc.vector.tensor_copy(v_w[1][:], tab_w[1][:].indirect(offsets[:]))
+        nc.vector.tensor_copy(
+            w2_s[:].rearrange("p (b t m) -> p b t m", b=2, t=4),
+            w2_s_raw[:].rearrange("p (b m t) -> p b t m", b=2, t=4),
+        )
+
+        def quantise_weight(raw, name, split):
+            rounded = ring.tile([P, 4 * PASS], BF16, name="w_rounded", align_bytes=64, bufs=3)
+            dst = rounded[:].rearrange("p (t m j) -> p m j t", t=4, j=4)
+            src = raw[:].rearrange("p j (m t) -> p m j t", t=4)
+            nc.scalar.copy(dst[:, 0:split], src[:, 0:split])
+            if split < P:
+                nc.vector.tensor_copy(dst[:, split:P], src[:, split:P])
+            codes = kept([P, PASS], U32, name + "_w")
+            scales = kept([P, PASS], U8, name + "_s")
+            nc.vector.quantize_mx(out=codes[:].bitcast(FP8X4), scales=scales[:], in_=rounded[:])
+            return codes, scales
+
+        w1_q = {}
+        w3_q = {}
+        h_q = {}
+
+        def stage1(b, jh, quant_w):
+            cols = slice(HALF * jh, HALF * (jh + 1))
+            held = ring.tile([P, 4, HALF], F32, name="held", align_bytes=64)
+            for t in range(4):
+                water = psum.tile([P, HALF], F32, name="water", bufs=4)
+                ch = slice(P * t, P * (t + 1))
+                for a in range(2):
+                    codes, scales = w1_q[b, a]
+                    nc.tensor.matmul_mx(
+                        out=water[:], lhsT=codes[:, ch].bitcast(FP8X4), lhsT_scale=scales[:, ch],
+                        rhs=v_w[a][:, cols].bitcast(FP8X4), rhs_scale=v_s[4 * a : P, cols],
+                        start=(a == 0), stop=(a == 1),
+                    )
+                src = water
+                if (b, jh, t) in VIA_SCALAR:
+                    src = ring.tile([P, HALF], F32, name="water_sb", align_bytes=64, bufs=4)
+                    nc.scalar.copy(src[:], water[:])
+                nc.vector.tensor_scalar(held[:, t, :], src[:], lo_sb[:, b, t : t + 1], hi_sb[:, b, t : t + 1], ALU.max, ALU.min)
+            return held
+
+        def stage1_tail(b, jh, held, start, width):
+            rounded = ring.tile([P, 4 * width], BF16, name="h_rounded", align_bytes=64, bufs=3)
+            for j0 in range(0, width, P):
+                lamp = psum.tile([P, 4, P], F32, name="lamp", bufs=2)
+                cols = slice(start + j0, start + j0 + P)
+                for t in range(4):
+                    c0 = PASS * b + P * t
+                    nc.tensor.matmul_mx(
+                        out=lamp[:, t, :], lhsT=w2_w[:, 2 * c0 : 2 * (c0 + P)].bitcast(FP4X4), lhsT_scale=w2_s[:, c0 : c0 + P],
+                        rhs=xs_w[:, cols].bitcast(FP8X4), rhs_scale=xs_s[:, cols], start=True, stop=True,
+                    )
+                h0 = start + j0 - HALF * jh
+                nc.vector.tensor_tensor(
+                    rounded[:, 4 * j0 : 4 * (j0 + P)].rearrange("p (c i t) -> p c t i", i=4, t=4),
+                    held[:, :, h0 : h0 + P].rearrange("p t (c i) -> p c t i", i=4),
+                    lamp[:].rearrange("p t (c i) -> p c t i", i=4),
+                    ALU.subtract,
+                )
+            codes = kept([P, width], U32, "h_w%d_%d" % (b, start))
+            scales = kept([P, width], U8, "h_s%d_%d" % (b, start))
+            nc.vector.quantize_mx(out=codes[:].bitcast(FP8X4), scales=scales[:], in_=rounded[:])
+            for j in range(start, start + width, P):
+                h_q[b, j] = (codes, scales, j - start)
+
+        y_s = kept([P, S], U8, "y_s")
+        y_rows = out_0.rearrange("(p t) s -> p t s", t=4)
+        y_words = out_1[0].rearrange("p c i -> p (c i)").bitcast(I32)
+
+        def stage2(start, width):
+            per_bank = 512 // width
+            y_sb = kept([P, 4, width], F32, "y_sb%d" % start)
+            for t0 in range(0, 4, per_bank):
+                acc = psum.tile([P, per_bank, width], F32, name="y_acc", bufs=2)
+                for t in range(t0, t0 + per_bank):
+                    ch = slice(P * t, P * (t + 1))
+                    for b in range(2):
+                        codes, scales = w3_q[b]
+                        h_codes, h_scales, h0 = h_q[b, start]
+                        nc.tensor.matmul_mx(
+                            out=acc[:, t - t0, :], lhsT=codes[:, ch].bitcast(FP8X4), lhsT_scale=scales[:, ch],
+                            rhs=h_codes[:, h0 : h0 + width].bitcast(FP8X4), rhs_scale=h_scales[:, h0 : h0 + width],
+                            start=(b == 0), stop=(b == 1),
+                        )
+                nc.scalar.copy(y_sb[:, t0 : t0 + per_bank, :], acc[:])
+            nc.sync.dma_start(y_rows[:, :, start : start + width], y_sb[:])
+            rounded = ring.tile([P, 4 * width], BF16, name="y_rounded", align_bytes=64)
+            dst = rounded[:].rearrange("p (c i t) -> p c t i", i=4, t=4)
+            src = y_sb[:].rearrange("p t (c i) -> p c t i", i=4)
+            if start in Y_CAST_ON_SCALAR:
+                nc.scalar.copy(dst, src)
+            else:
+                nc.vector.tensor_copy(dst, src)
+            codes = kept([P, width], U32, "y_w%d" % start)
+            nc.vector.quantize_mx(out=codes[:].bitcast(FP8X4), scales=y_s[:, start : start + width], in_=rounded[:])
+            nc.sync.dma_start(y_words[:, start : start + width], codes[:].bitcast(I32))
+
+        w1_q[0, 0] = quantise_weight(w1_raw[0][0], "w1_00", P)
+        w1_q[0, 1] = quantise_weight(w1_raw[0][1], "w1_01", 48)
+        held = stage1(0, 0, None)
+        stage1_tail(0, 0, held, 0, HALF)
+        w1_q[1, 0] = quantise_weight(w1_raw[1][0], "w1_10", P)
+        held = stage1(0, 1, None)
+        w1_q[1, 1] = quantise_weight(w1_raw[1][1], "w1_11", P)
+        stage1_tail(0, 1, held, HALF, HALF)
+        held_by_half = [stage1(1, 0, None)]
+        w3_q[0] = quantise_weight(w3_raw[0], "w3_0", P)
+        w3_q[1] = quantise_weight(w3_raw[1], "w3_1", P)
+        previous = None
+        for start, width in Y_CHUNKS:
+            if start == HALF:
+                held_by_half.append(stage1(1, 1, None))
+            stage1_tail(1, start // HALF, held_by_half[start // HALF], start, width)
+            if previous is not None:
+                stage2(*previous)
+            previous = (start, width)
+        stage2(*previous)
+        for q in range(4):
+            nc.sync.dma_start(out_2[0, 4 * q : 4 * q + 4, :].bitcast(I32), y_s[32 * q : 32 * q + 4, :].bitcast(I32))

@@ -18,9 +18,10 @@ ALU = mybir.AluOpType
 P = 128
 PASS = 512
 HALF = 512
-VIA_SCALAR = {(0, 0, 3), (0, 1, 2), (0, 1, 3), (1, 0, 2), (1, 0, 3), (1, 1, 1), (1, 1, 2), (1, 1, 3)}
+SLOT = 8192
+VIA_SCALAR = {(0, 0, 1), (0, 0, 3), (0, 1, 1), (0, 1, 3), (1, 0, 1), (1, 0, 2), (1, 0, 3), (1, 1, 0), (1, 1, 1), (1, 1, 2), (1, 1, 3)}
 Y_CHUNKS = ((0, 256), (256, 256), (512, 256), (768, 128), (896, 128))
-Y_CAST_ON_SCALAR = (0, 256)
+Y_CAST_ON_SCALAR = (0, 256, 512)
 
 
 def tile_list_ballast_kill_encoder_kernel(
@@ -29,79 +30,85 @@ def tile_list_ballast_kill_encoder_kernel(
     nc = tc.nc
     with ExitStack() as ctx:
         keep = ctx.enter_context(tc.tile_pool(name="keep", bufs=1))
+        stage = ctx.enter_context(tc.tile_pool(name="stage", bufs=1))
         ring = ctx.enter_context(tc.tile_pool(name="ring", bufs=2))
         psum = ctx.enter_context(tc.psum_pool(name="psum", bufs=1))
 
         def kept(shape, dtype, name):
             return keep.tile(shape, dtype, name=name, align_bytes=64)
 
+        def staged(shape, dtype, name, offset):
+            return stage.tile(shape, dtype, name=name, offset=offset, align_bytes=64)
+
         offsets = kept([P, S // 16], U16, "offsets")
-        tab_w = [kept([P, T], U32, "tab_w%d" % a) for a in range(2)]
         tab_s = kept([P, T], U8, "tab_s")
-        xs_w = kept([P, S], U32, "xs_w")
         xs_s = kept([P, S], U8, "xs_s")
-        w2_raw = kept([P, 2 * H], U8, "w2_raw")
-        w2_s_raw = kept([P, H], U8, "w2_s_raw")
         lo_sb = kept([P, 2, 4], F32, "lo_sb")
         hi_sb = kept([P, 2, 4], F32, "hi_sb")
-        w1_raw = [[kept([P, 4, PASS], F32, "w1_raw%d%d" % (b, a)) for a in range(2)] for b in range(2)]
-        w3_raw = [kept([P, 4, N], F32, "w3_raw%d" % b) for b in range(2)]
+        w2_w = kept([P, 2 * H], U8, "w2_w")
+        w2_s = kept([P, H], U8, "w2_s")
+        v_w = [kept([P, S], U32, "v_w%d" % a) for a in range(2)]
+        v_s = kept([P, S], U8, "v_s")
 
-        for plane in (tab_s, w2_s_raw, xs_s):
-            nc.vector.memset(plane[:].bitcast(I32), 0)
+        def load_rows(rows, name, offset):
+            raw = staged([P, 4, PASS], F32, name, offset)
+            nc.sync.dma_start(raw[:], rows.rearrange("(p j) c -> p j c", j=4))
+            return raw
 
-        def load_w1(b, a):
-            rows = w1[PASS * a : PASS * (a + 1), PASS * b : PASS * (b + 1)]
-            nc.sync.dma_start(w1_raw[b][a][:], rows.rearrange("(p j) c -> p j c", j=4))
+        def load_w1(b, a, offset):
+            return load_rows(w1[PASS * a : PASS * (a + 1), PASS * b : PASS * (b + 1)], "w1_raw%d%d" % (b, a), offset)
 
-        def load_words(tile, words):
+        def load_words(words, name, offset):
+            tile = staged([P, words.shape[1]], U32, name, offset)
             nc.sync.dma_start(tile[:].bitcast(I32), words.rearrange("p c i -> p (c i)").bitcast(I32))
+            return tile
 
-        load_words(tab_w[0], tab_words[0])
+        w2_raw = staged([P, 2 * H], U8, "w2_raw", 2 * SLOT)
+        w2_s_raw = staged([P, H], U8, "w2_s_raw", 4 * SLOT)
+        for plane in (w2_s_raw, tab_s, xs_s):
+            nc.vector.memset(plane[:].bitcast(I32), 0)
         nc.sync.dma_start(offsets[:], offs)
-        for q in range(4):
-            nc.sync.dma_start(tab_s[32 * q : 32 * q + 8, :].bitcast(I32), tab_scales[:, 4 * q : 4 * q + 4, :].bitcast(I32))
-        nc.scalar.dma_start(w2_raw[:].bitcast(I32), w2_words[0].bitcast(I32))
-        load_words(tab_w[1], tab_words[1])
-        load_w1(0, 0)
-        load_w1(0, 1)
-        load_words(xs_w, xs_words[0])
-        load_w1(1, 0)
-        load_w1(1, 1)
-        for b in range(2):
-            nc.sync.dma_start(w3_raw[b][:], w3[PASS * b : PASS * (b + 1), :].rearrange("(p j) n -> p j n", j=4))
-
-        for q in range(4):
-            nc.gpsimd.dma_start(w2_s_raw[32 * q : 32 * q + 4, :].bitcast(I32), w2_scales[0, 4 * q : 4 * q + 4, :].bitcast(I32))
+        nc.sync.dma_start(w2_raw[:].bitcast(I32), w2_words[0].bitcast(I32))
+        tab_w0 = load_words(tab_words[0], "tab_w0", 0)
         nc.gpsimd.dma_start(lo_sb[:], lo.rearrange("(b p t) -> p b t", b=2, t=4))
         nc.gpsimd.dma_start(hi_sb[:], hi.rearrange("(b p t) -> p b t", b=2, t=4))
         for q in range(4):
+            nc.scalar.dma_start(w2_s_raw[32 * q : 32 * q + 4, :].bitcast(I32), w2_scales[0, 4 * q : 4 * q + 4, :].bitcast(I32))
+        for q in range(4):
+            for a in range(2):
+                rows = slice(32 * q + 4 * a, 32 * q + 4 * a + 4)
+                nc.scalar.dma_start(tab_s[rows, :].bitcast(I32), tab_scales[a, 4 * q : 4 * q + 4, :].bitcast(I32))
+        for q in range(4):
             nc.gpsimd.dma_start(xs_s[32 * q : 32 * q + 4, :].bitcast(I32), xs_scales[0, 4 * q : 4 * q + 4, :].bitcast(I32))
 
-        w2_w = kept([P, 2 * H], U8, "w2_w")
-        w2_s = kept([P, H], U8, "w2_s")
         nc.vector.tensor_copy(
             w2_w[:].rearrange("p (b t m e) -> p b t m e", b=2, t=4, e=2),
             w2_raw[:].rearrange("p (b m t e) -> p b t m e", b=2, t=4, e=2),
         )
-
-        v_w = [kept([P, S], U32, "v_w%d" % a) for a in range(2)]
-        v_s = kept([P, S], U8, "v_s")
-        nc.vector.tensor_copy(v_w[0][:], tab_w[0][:].indirect(offsets[:]))
-        nc.vector.tensor_copy(v_s[:], tab_s[:].indirect(offsets[:]))
-        nc.vector.tensor_copy(v_w[1][:], tab_w[1][:].indirect(offsets[:]))
+        tab_w1 = load_words(tab_words[1], "tab_w1", 2 * SLOT)
         nc.vector.tensor_copy(
             w2_s[:].rearrange("p (b t m) -> p b t m", b=2, t=4),
             w2_s_raw[:].rearrange("p (b m t) -> p b t m", b=2, t=4),
         )
+        w1_raw = {}
+        w1_raw[0, 0] = load_w1(0, 0, 4 * SLOT)
+        nc.vector.tensor_copy(v_w[0][:], tab_w0[:].indirect(offsets[:]))
+        w1_raw[0, 1] = load_w1(0, 1, 0)
+        xs_w = load_words(xs_words[0], "xs_w", SLOT)
+        nc.vector.tensor_copy(v_s[:], tab_s[:].indirect(offsets[:]))
+        nc.vector.tensor_copy(v_w[1][:], tab_w1[:].indirect(offsets[:]))
+        w1_raw[1, 0] = load_w1(1, 0, 2 * SLOT)
+        w1_raw[1, 1] = load_w1(1, 1, 3 * SLOT)
 
-        def quantise_weight(raw, name, split):
+        def quantise_weight(raw, name, split=P // 2, on_vector=False):
             rounded = ring.tile([P, 4 * PASS], BF16, name="w_rounded", align_bytes=64, bufs=3)
             dst = rounded[:].rearrange("p (t m j) -> p m j t", t=4, j=4)
             src = raw[:].rearrange("p j (m t) -> p m j t", t=4)
             nc.scalar.copy(dst[:, 0:split], src[:, 0:split])
-            if split < P:
+            if on_vector:
                 nc.vector.tensor_copy(dst[:, split:P], src[:, split:P])
+            else:
+                nc.scalar.copy(dst[:, split:P], src[:, split:P])
             codes = kept([P, PASS], U32, name + "_w")
             scales = kept([P, PASS], U8, name + "_s")
             nc.vector.quantize_mx(out=codes[:].bitcast(FP8X4), scales=scales[:], in_=rounded[:])
@@ -160,44 +167,49 @@ def tile_list_ballast_kill_encoder_kernel(
         y_words = out_1[0].rearrange("p c i -> p (c i)").bitcast(I32)
 
         def stage2(start, width):
+            last = start + width == S
             per_bank = 512 // width
             y_sb = kept([P, 4, width], F32, "y_sb%d" % start)
+            rounded = ring.tile([P, 4 * width], BF16, name="y_rounded", align_bytes=64)
+            dst = rounded[:].rearrange("p (c i t) -> p c t i", i=4, t=4)
             for t0 in range(0, 4, per_bank):
                 acc = psum.tile([P, per_bank, width], F32, name="y_acc", bufs=2)
-                for t in range(t0, t0 + per_bank):
-                    ch = slice(P * t, P * (t + 1))
-                    for b in range(2):
-                        codes, scales = w3_q[b]
-                        h_codes, h_scales, h0 = h_q[b, start]
+                for b in range(2):
+                    codes, scales = w3_q[b]
+                    h_codes, h_scales, h0 = h_q[b, start]
+                    for t in range(t0, t0 + per_bank):
+                        ch = slice(P * t, P * (t + 1))
                         nc.tensor.matmul_mx(
                             out=acc[:, t - t0, :], lhsT=codes[:, ch].bitcast(FP8X4), lhsT_scale=scales[:, ch],
                             rhs=h_codes[:, h0 : h0 + width].bitcast(FP8X4), rhs_scale=h_scales[:, h0 : h0 + width],
-                            start=(b == 0), stop=(b == 1),
+                            start=(b == 0 and t == t0), stop=(b == 1 and t == t0 + per_bank - 1),
                         )
+                if last:
+                    nc.vector.tensor_copy(dst, acc[:].rearrange("p t (c i) -> p c t i", i=4))
                 nc.scalar.copy(y_sb[:, t0 : t0 + per_bank, :], acc[:])
-            nc.sync.dma_start(y_rows[:, :, start : start + width], y_sb[:])
-            rounded = ring.tile([P, 4 * width], BF16, name="y_rounded", align_bytes=64)
-            dst = rounded[:].rearrange("p (c i t) -> p c t i", i=4, t=4)
+            queue = nc.scalar if last else nc.sync
+            queue.dma_start(y_rows[:, :, start : start + width], y_sb[:])
             src = y_sb[:].rearrange("p t (c i) -> p c t i", i=4)
             if start in Y_CAST_ON_SCALAR:
                 nc.scalar.copy(dst, src)
-            else:
+            elif not last:
                 nc.vector.tensor_copy(dst, src)
             codes = kept([P, width], U32, "y_w%d" % start)
             nc.vector.quantize_mx(out=codes[:].bitcast(FP8X4), scales=y_s[:, start : start + width], in_=rounded[:])
             nc.sync.dma_start(y_words[:, start : start + width], codes[:].bitcast(I32))
 
-        w1_q[0, 0] = quantise_weight(w1_raw[0][0], "w1_00", P)
-        w1_q[0, 1] = quantise_weight(w1_raw[0][1], "w1_01", 48)
+        w1_q[0, 0] = quantise_weight(w1_raw[0, 0], "w1_00", 64, True)
+        w1_q[0, 1] = quantise_weight(w1_raw[0, 1], "w1_01", 44, True)
+        w3_raw = [load_rows(w3[PASS * b : PASS * (b + 1), :], "w3_raw%d" % b, offset) for b, offset in enumerate((4 * SLOT, 0))]
         held = stage1(0, 0, None)
         stage1_tail(0, 0, held, 0, HALF)
-        w1_q[1, 0] = quantise_weight(w1_raw[1][0], "w1_10", P)
+        w1_q[1, 0] = quantise_weight(w1_raw[1, 0], "w1_10")
         held = stage1(0, 1, None)
-        w1_q[1, 1] = quantise_weight(w1_raw[1][1], "w1_11", P)
+        w1_q[1, 1] = quantise_weight(w1_raw[1, 1], "w1_11")
         stage1_tail(0, 1, held, HALF, HALF)
         held_by_half = [stage1(1, 0, None)]
-        w3_q[0] = quantise_weight(w3_raw[0], "w3_0", P)
-        w3_q[1] = quantise_weight(w3_raw[1], "w3_1", P)
+        w3_q[0] = quantise_weight(w3_raw[0], "w3_0")
+        w3_q[1] = quantise_weight(w3_raw[1], "w3_1")
         previous = None
         for start, width in Y_CHUNKS:
             if start == HALF:
@@ -208,4 +220,4 @@ def tile_list_ballast_kill_encoder_kernel(
             previous = (start, width)
         stage2(*previous)
         for q in range(4):
-            nc.sync.dma_start(out_2[0, 4 * q : 4 * q + 4, :].bitcast(I32), y_s[32 * q : 32 * q + 4, :].bitcast(I32))
+            (nc.sync if q < 2 else nc.scalar).dma_start(out_2[0, 4 * q : 4 * q + 4, :].bitcast(I32), y_s[32 * q : 32 * q + 4, :].bitcast(I32))

from contextlib import ExitStack

import concourse.mybir as mybir

K, K2, H, N, T, S = 1024, 512, 1024, 512, 4096, 1024
FLOPS = 2 * S * (K * H + K2 * H + H * N)

F32 = mybir.dt.float32
BF16 = mybir.dt.bfloat16
I32 = mybir.dt.int32
U32 = mybir.dt.uint32
U16 = mybir.dt.uint16
U8 = mybir.dt.uint8
FP8X4 = mybir.dt.float8_e4m3fn_x4
FP4X4 = mybir.dt.float4_e2m1fn_x4
ALU = mybir.AluOpType

P = 128
PASS = 512
HALF = 512
SLOT = 8192
VIA_SCALAR = {(0, 0, 1), (0, 0, 3), (0, 1, 1), (0, 1, 3), (1, 0, 1), (1, 0, 2), (1, 0, 3), (1, 1, 0), (1, 1, 1), (1, 1, 2), (1, 1, 3)}
Y_CHUNKS = ((0, 256), (256, 256), (512, 256), (768, 128), (896, 128))
Y_CAST_ON_SCALAR = (0, 256, 512)


def tile_list_ballast_kill_encoder_kernel(
    tc, tab_words, tab_scales, offs, xs_words, xs_scales, w1, w2_words, w2_scales, lo, hi, w3, out_0, out_1, out_2
):
    nc = tc.nc
    with ExitStack() as ctx:
        keep = ctx.enter_context(tc.tile_pool(name="keep", bufs=1))
        stage = ctx.enter_context(tc.tile_pool(name="stage", bufs=1))
        ring = ctx.enter_context(tc.tile_pool(name="ring", bufs=2))
        psum = ctx.enter_context(tc.psum_pool(name="psum", bufs=1))

        def kept(shape, dtype, name):
            return keep.tile(shape, dtype, name=name, align_bytes=64)

        def staged(shape, dtype, name, offset):
            return stage.tile(shape, dtype, name=name, offset=offset, align_bytes=64)

        offsets = kept([P, S // 16], U16, "offsets")
        tab_s = kept([P, T], U8, "tab_s")
        xs_s = kept([P, S], U8, "xs_s")
        lo_sb = kept([P, 2, 4], F32, "lo_sb")
        hi_sb = kept([P, 2, 4], F32, "hi_sb")
        w2_w = kept([P, 2 * H], U8, "w2_w")
        w2_s = kept([P, H], U8, "w2_s")
        v_w = [kept([P, S], U32, "v_w%d" % a) for a in range(2)]
        v_s = kept([P, S], U8, "v_s")

        def load_rows(rows, name, offset):
            raw = staged([P, 4, PASS], F32, name, offset)
            nc.sync.dma_start(raw[:], rows.rearrange("(p j) c -> p j c", j=4))
            return raw

        def load_w1(b, a, offset):
            return load_rows(w1[PASS * a : PASS * (a + 1), PASS * b : PASS * (b + 1)], "w1_raw%d%d" % (b, a), offset)

        def load_words(words, name, offset):
            tile = staged([P, words.shape[1]], U32, name, offset)
            nc.sync.dma_start(tile[:].bitcast(I32), words.rearrange("p c i -> p (c i)").bitcast(I32))
            return tile

        w2_raw = staged([P, 2 * H], U8, "w2_raw", 2 * SLOT)
        w2_s_raw = staged([P, H], U8, "w2_s_raw", 4 * SLOT)
        for plane in (w2_s_raw, tab_s, xs_s):
            nc.vector.memset(plane[:].bitcast(I32), 0)
        nc.sync.dma_start(offsets[:], offs)
        nc.sync.dma_start(w2_raw[:].bitcast(I32), w2_words[0].bitcast(I32))
        tab_w0 = load_words(tab_words[0], "tab_w0", 0)
        nc.gpsimd.dma_start(lo_sb[:], lo.rearrange("(b p t) -> p b t", b=2, t=4))
        nc.gpsimd.dma_start(hi_sb[:], hi.rearrange("(b p t) -> p b t", b=2, t=4))
        for q in range(4):
            nc.scalar.dma_start(w2_s_raw[32 * q : 32 * q + 4, :].bitcast(I32), w2_scales[0, 4 * q : 4 * q + 4, :].bitcast(I32))
        for q in range(4):
            for a in range(2):
                rows = slice(32 * q + 4 * a, 32 * q + 4 * a + 4)
                nc.scalar.dma_start(tab_s[rows, :].bitcast(I32), tab_scales[a, 4 * q : 4 * q + 4, :].bitcast(I32))
        for q in range(4):
            nc.gpsimd.dma_start(xs_s[32 * q : 32 * q + 4, :].bitcast(I32), xs_scales[0, 4 * q : 4 * q + 4, :].bitcast(I32))

        nc.vector.tensor_copy(
            w2_w[:].rearrange("p (b t m e) -> p b t m e", b=2, t=4, e=2),
            w2_raw[:].rearrange("p (b m t e) -> p b t m e", b=2, t=4, e=2),
        )
        tab_w1 = load_words(tab_words[1], "tab_w1", 2 * SLOT)
        nc.vector.tensor_copy(
            w2_s[:].rearrange("p (b t m) -> p b t m", b=2, t=4),
            w2_s_raw[:].rearrange("p (b m t) -> p b t m", b=2, t=4),
        )
        w1_raw = {}
        w1_raw[0, 0] = load_w1(0, 0, 4 * SLOT)
        nc.vector.tensor_copy(v_w[0][:], tab_w0[:].indirect(offsets[:]))
        w1_raw[0, 1] = load_w1(0, 1, 0)
        xs_w = load_words(xs_words[0], "xs_w", SLOT)
        nc.vector.tensor_copy(v_s[:], tab_s[:].indirect(offsets[:]))
        nc.vector.tensor_copy(v_w[1][:], tab_w1[:].indirect(offsets[:]))
        w1_raw[1, 0] = load_w1(1, 0, 2 * SLOT)
        w1_raw[1, 1] = load_w1(1, 1, 3 * SLOT)

        def quantise_weight(raw, name, split=P // 2, on_vector=False):
            rounded = ring.tile([P, 4 * PASS], BF16, name="w_rounded", align_bytes=64, bufs=3)
            dst = rounded[:].rearrange("p (t m j) -> p m j t", t=4, j=4)
            src = raw[:].rearrange("p j (m t) -> p m j t", t=4)
            nc.scalar.copy(dst[:, 0:split], src[:, 0:split])
            if on_vector:
                nc.vector.tensor_copy(dst[:, split:P], src[:, split:P])
            else:
                nc.scalar.copy(dst[:, split:P], src[:, split:P])
            codes = kept([P, PASS], U32, name + "_w")
            scales = kept([P, PASS], U8, name + "_s")
            nc.vector.quantize_mx(out=codes[:].bitcast(FP8X4), scales=scales[:], in_=rounded[:])
            return codes, scales

        w1_q = {}
        w3_q = {}
        h_q = {}

        def stage1(b, jh, quant_w):
            cols = slice(HALF * jh, HALF * (jh + 1))
            held = ring.tile([P, 4, HALF], F32, name="held", align_bytes=64)
            for t in range(4):
                water = psum.tile([P, HALF], F32, name="water", bufs=4)
                ch = slice(P * t, P * (t + 1))
                for a in range(2):
                    codes, scales = w1_q[b, a]
                    nc.tensor.matmul_mx(
                        out=water[:], lhsT=codes[:, ch].bitcast(FP8X4), lhsT_scale=scales[:, ch],
                        rhs=v_w[a][:, cols].bitcast(FP8X4), rhs_scale=v_s[4 * a : P, cols],
                        start=(a == 0), stop=(a == 1),
                    )
                src = water
                if (b, jh, t) in VIA_SCALAR:
                    src = ring.tile([P, HALF], F32, name="water_sb", align_bytes=64, bufs=4)
                    nc.scalar.copy(src[:], water[:])
                nc.vector.tensor_scalar(held[:, t, :], src[:], lo_sb[:, b, t : t + 1], hi_sb[:, b, t : t + 1], ALU.max, ALU.min)
            return held

        def stage1_tail(b, jh, held, start, width):
            rounded = ring.tile([P, 4 * width], BF16, name="h_rounded", align_bytes=64, bufs=3)
            for j0 in range(0, width, P):
                lamp = psum.tile([P, 4, P], F32, name="lamp", bufs=2)
                cols = slice(start + j0, start + j0 + P)
                for t in range(4):
                    c0 = PASS * b + P * t
                    nc.tensor.matmul_mx(
                        out=lamp[:, t, :], lhsT=w2_w[:, 2 * c0 : 2 * (c0 + P)].bitcast(FP4X4), lhsT_scale=w2_s[:, c0 : c0 + P],
                        rhs=xs_w[:, cols].bitcast(FP8X4), rhs_scale=xs_s[:, cols], start=True, stop=True,
                    )
                h0 = start + j0 - HALF * jh
                nc.vector.tensor_tensor(
                    rounded[:, 4 * j0 : 4 * (j0 + P)].rearrange("p (c i t) -> p c t i", i=4, t=4),
                    held[:, :, h0 : h0 + P].rearrange("p t (c i) -> p c t i", i=4),
                    lamp[:].rearrange("p t (c i) -> p c t i", i=4),
                    ALU.subtract,
                )
            codes = kept([P, width], U32, "h_w%d_%d" % (b, start))
            scales = kept([P, width], U8, "h_s%d_%d" % (b, start))
            nc.vector.quantize_mx(out=codes[:].bitcast(FP8X4), scales=scales[:], in_=rounded[:])
            for j in range(start, start + width, P):
                h_q[b, j] = (codes, scales, j - start)

        y_s = kept([P, S], U8, "y_s")
        y_rows = out_0.rearrange("(p t) s -> p t s", t=4)
        y_words = out_1[0].rearrange("p c i -> p (c i)").bitcast(I32)

        def stage2(start, width):
            last = start + width == S
            per_bank = 512 // width
            y_sb = kept([P, 4, width], F32, "y_sb%d" % start)
            rounded = ring.tile([P, 4 * width], BF16, name="y_rounded", align_bytes=64)
            dst = rounded[:].rearrange("p (c i t) -> p c t i", i=4, t=4)
            for t0 in range(0, 4, per_bank):
                acc = psum.tile([P, per_bank, width], F32, name="y_acc", bufs=2)
                for b in range(2):
                    codes, scales = w3_q[b]
                    h_codes, h_scales, h0 = h_q[b, start]
                    for t in range(t0, t0 + per_bank):
                        ch = slice(P * t, P * (t + 1))
                        nc.tensor.matmul_mx(
                            out=acc[:, t - t0, :], lhsT=codes[:, ch].bitcast(FP8X4), lhsT_scale=scales[:, ch],
                            rhs=h_codes[:, h0 : h0 + width].bitcast(FP8X4), rhs_scale=h_scales[:, h0 : h0 + width],
                            start=(b == 0 and t == t0), stop=(b == 1 and t == t0 + per_bank - 1),
                        )
                if last:
                    nc.vector.tensor_copy(dst, acc[:].rearrange("p t (c i) -> p c t i", i=4))
                nc.scalar.copy(y_sb[:, t0 : t0 + per_bank, :], acc[:])
            queue = nc.scalar if last else nc.sync
            queue.dma_start(y_rows[:, :, start : start + width], y_sb[:])
            src = y_sb[:].rearrange("p t (c i) -> p c t i", i=4)
            if start in Y_CAST_ON_SCALAR:
                nc.scalar.copy(dst, src)
            elif not last:
                nc.vector.tensor_copy(dst, src)
            codes = kept([P, width], U32, "y_w%d" % start)
            nc.vector.quantize_mx(out=codes[:].bitcast(FP8X4), scales=y_s[:, start : start + width], in_=rounded[:])
            nc.sync.dma_start(y_words[:, start : start + width], codes[:].bitcast(I32))

        w1_q[0, 0] = quantise_weight(w1_raw[0, 0], "w1_00", 64, True)
        w1_q[0, 1] = quantise_weight(w1_raw[0, 1], "w1_01", 44, True)
        w3_raw = [load_rows(w3[PASS * b : PASS * (b + 1), :], "w3_raw%d" % b, offset) for b, offset in enumerate((4 * SLOT, 0))]
        held = stage1(0, 0, None)
        stage1_tail(0, 0, held, 0, HALF)
        w1_q[1, 0] = quantise_weight(w1_raw[1, 0], "w1_10")
        held = stage1(0, 1, None)
        w1_q[1, 1] = quantise_weight(w1_raw[1, 1], "w1_11")
        stage1_tail(0, 1, held, HALF, HALF)
        held_by_half = [stage1(1, 0, None)]
        w3_q[0] = quantise_weight(w3_raw[0], "w3_0")
        w3_q[1] = quantise_weight(w3_raw[1], "w3_1")
        previous = None
        for start, width in Y_CHUNKS:
            if start == HALF:
                held_by_half.append(stage1(1, 1, None))
            stage1_tail(1, start // HALF, held_by_half[start // HALF], start, width)
            if previous is not None:
                stage2(*previous)
            previous = (start, width)
        stage2(*previous)
        for q in range(4):
            (nc.sync if q < 2 else nc.scalar).dma_start(out_2[0, 4 * q : 4 * q + 4, :].bitcast(I32), y_s[32 * q : 32 * q + 4, :].bitcast(I32))
